import numpy as np
import ml_dtypes


def mxq(x, axis, fmt="e4m3"):
    dtype, down = {"e4m3": (ml_dtypes.float8_e4m3fn, 7), "e5m2": (ml_dtypes.float8_e5m2, 14)}[fmt]
    v = np.moveaxis(np.asarray(x, np.float32).astype(ml_dtypes.bfloat16).astype(np.float64), axis, -1)
    blocks = v.reshape(v.shape[:-1] + (-1, 32))
    amax = np.abs(blocks).max(-1, keepdims=True)
    byte = np.maximum(np.where(amax > 0, np.frexp(amax)[1] - 1 + 127, 0) - down, 1)
    scale = np.exp2(byte - 127.0)
    codes = (blocks / scale).astype(np.float32).astype(dtype).astype(np.float64)
    return np.moveaxis((codes * scale).reshape(v.shape), -1, axis)


WIDE = False


def mx_kscale(k):
    if not WIDE:
        return np.ones(k)
    levels = np.array([10, -10, 5, -5, 0])
    if k % 512:
        return np.exp2(np.random.permutation(np.resize(levels, k // 32))).repeat(32)
    a = np.empty((k // 512, 16))
    for p in range(k // 512):
        a[p, :8] = np.random.permutation(np.resize(levels, 8))
        for g in range(8):
            far = levels[np.abs(levels - a[p, g]) >= 10]
            a[p, g + 8] = far[np.random.randint(len(far))]
    return np.exp2(a.ravel()).repeat(32)


def f64(x):
    return np.asarray(x).astype(np.float64)


E2M1 = np.array([0.0, 0.5, 1.0, 1.5, 2.0, 3.0, 4.0, 6.0, -0.0, -0.5, -1.0, -1.5, -2.0, -3.0, -4.0, -6.0])


def pack_weight(w, fmt):
    k, n = w.shape
    w = f64(np.asarray(w, np.float32).astype(ml_dtypes.bfloat16)).reshape(k // 32, 32, n)
    amax = np.abs(w).max(1)
    if fmt == "e4m3":
        byte = np.frexp(amax)[1] - 1 + 127 - 7
    else:
        mant, ex = np.frexp(amax / 6.0)
        byte = np.where(mant > 0.5, ex, ex - 1) + 127
    byte = np.clip(np.where(amax > 0, byte, 1), 1, 254)
    scaled = (w * np.exp2(127.0 - byte)[:, None, :]).reshape(k, n).astype(np.float32)
    by_word = np.ascontiguousarray(scaled.reshape(k // 512, 128, 4, n).transpose(0, 1, 3, 2))
    if fmt == "e4m3":
        words = by_word.astype(ml_dtypes.float8_e4m3fn).view(np.uint8)
    else:
        c = by_word.astype(ml_dtypes.float4_e2m1fn).view(np.uint8) & 0xF
        words = (c[..., 0::2] | (c[..., 1::2] << 4)).reshape(k // 512, 128, 2 * n)
    return np.ascontiguousarray(words), np.ascontiguousarray(byte.astype(np.uint8).reshape(k // 512, 16, n))


def unpack_weight(words, scales, fmt):
    g, _, n = scales.shape
    words = np.ascontiguousarray(words).reshape(g, 128, n, -1)
    if fmt == "e4m3":
        vals = words.view(ml_dtypes.float8_e4m3fn).astype(np.float64)
    else:
        nib = np.empty((g, 128, n, 4), np.uint8)
        nib[..., 0::2] = words & 0xF
        nib[..., 1::2] = words >> 4
        vals = E2M1[nib]
    vals = vals * np.repeat(np.exp2(scales.astype(np.float64) - 127.0), 8, axis=1)[..., None]
    return vals.transpose(0, 1, 3, 2).reshape(g * 512, n)


def planes(y):
    n, m = y.shape
    v = y.astype(np.float32).astype(ml_dtypes.bfloat16).astype(np.float64).reshape(n // 32, 32, m)
    top = np.abs(v).max(1)
    byte = np.clip(np.where(top > 0, np.frexp(top)[1] - 1 + 127 - 7, 1), 1, 254)
    codes = (v * np.exp2(127.0 - byte)[:, None, :]).reshape(n, m).astype(np.float32).astype(ml_dtypes.float8_e4m3fn).view(np.uint8)
    words = codes.reshape(n // 512, 128, 4, m).transpose(0, 1, 3, 2)
    return np.ascontiguousarray(words), np.ascontiguousarray(byte.astype(np.uint8).reshape(n // 512, 16, m))


K, M, T = 1024, 512, 512


def setup_inputs():
    n = np.random.standard_normal
    s = mx_kscale(K)[:, None]
    x = n((K, T)) * s
    x4 = pack_weight(x, "e2m1")
    rest = x - unpack_weight(*x4, "e2m1")
    p_w4 = pack_weight(n((K, M)) / np.sqrt(K) / s, "e2m1")
    return {
        "x4_words": x4[0],
        "x4_scales": x4[1],
        "xr": (rest).astype(np.float32),
        "w4_words": p_w4[0],
        "w4_scales": p_w4[1],
    }


def reference(x4_words, x4_scales, xr, w4_words, w4_scales):
    x4_ = unpack_weight(x4_words, x4_scales, "e2m1")
    xr_ = mxq(f64(xr), 0, "e4m3")
    w4_ = unpack_weight(w4_words, w4_scales, "e2m1")
    y = x4_.T @ w4_ + xr_.T @ w4_
    out_0 = np.maximum(y, 0.0) ** 2
    return (out_0,) + planes(out_0)

@@ -1,0 +1,151 @@
+from contextlib import ExitStack
+
+import concourse.mybir as mybir
+
+K, T, N = 1024, 512, 512
+FLOPS = 2 * 2 * K * T * N
+
+F32 = mybir.dt.float32
+BF16 = mybir.dt.bfloat16
+I32 = mybir.dt.int32
+U32 = mybir.dt.uint32
+U8 = mybir.dt.uint8
+FP8X4 = mybir.dt.float8_e4m3fn_x4
+FP4X4 = mybir.dt.float4_e2m1fn_x4
+ALU = mybir.AluOpType
+ACT = mybir.ActivationFunctionType
+
+P = 128
+PACK = 4
+PASSES = K // (P * PACK)
+QUADS = 4
+XR_SPLIT = 84
+OUT_SPLIT = 168
+
+
+def tile_mix_xres_tm_pl_relu2_kernel(
+    tc, x4_words, x4_scales, xr, w4_words, w4_scales, out_0, out_1, out_2
+):
+    nc = tc.nc
+    with ExitStack() as ctx:
+        sb = ctx.enter_context(tc.tile_pool(name="sb", bufs=1))
+        psum = ctx.enter_context(tc.psum_pool(name="psum", bufs=1))
+        ctx.enter_context(tc.manual_schedule())
+
+        x4_raw = sb.tile([P, PASSES, 2 * T], U8, align_bytes=64)
+        x4s_raw = sb.tile([P, PASSES, T], U8, align_bytes=64)
+        w4 = sb.tile([P, PASSES, 2 * N], U8, align_bytes=64)
+        w4s = sb.tile([P, PASSES, N], U8, align_bytes=64)
+        x4 = [sb.tile([P, PACK, 2 * P], U8, align_bytes=64, name="x4_%d" % a) for a in range(PASSES)]
+        x4s = sb.tile([P, PASSES, PACK, P], U8, align_bytes=64)
+        xr0_raw = sb.tile([P, PACK, T], F32, align_bytes=64)
+        xr1_raw = [sb.tile([P, 2, T], F32, align_bytes=64, name="xr1_raw_%d" % u) for u in range(2)]
+        xr_bf = [sb.tile([P, PACK, P, PACK], BF16, align_bytes=64, name="xr_bf_%d" % a) for a in range(PASSES)]
+        xq = [sb.tile([P, PACK, P], U32, align_bytes=64, name="xq_%d" % a) for a in range(PASSES)]
+        xqs = [sb.tile([P, PACK, P], U8, align_bytes=64, name="xqs_%d" % a) for a in range(PASSES)]
+        acc = [psum.tile([P, N], F32, name="acc_%d" % r) for r in range(PACK)]
+        pos = [sb.tile([P, N], F32, align_bytes=64, name="pos_%d" % r) for r in range(PACK)]
+        res = sb.tile([P, PACK, N], F32, align_bytes=64)
+        res_bf = [sb.tile([P, N // 2, PACK], BF16, align_bytes=64, name="res_bf_%d" % h) for h in range(2)]
+        codes = sb.tile([P, N], U32, align_bytes=64)
+        scales = sb.tile([P, N], U8, align_bytes=64)
+
+        def load_scale_rows(plane, rows):
+            for q in range(QUADS):
+                nc.scalar.dma_start(
+                    out=plane[32 * q : 32 * q + 4, :, :].bitcast(I32),
+                    in_=rows[:, 4 * q : 4 * q + 4, :].rearrange("a s c -> s a c").bitcast(I32),
+                )
+
+        nc.vector.memset(x4s_raw[:].bitcast(U32), 0)
+        nc.vector.memset(w4s[:].bitcast(U32), 0)
+
+        nc.sync.dma_start(out=x4_raw[:].bitcast(I32), in_=x4_words.rearrange("a p c -> p a c").bitcast(I32))
+        nc.sync.dma_start(out=w4[:].bitcast(I32), in_=w4_words.rearrange("a p c -> p a c").bitcast(I32))
+        load_scale_rows(x4s_raw, x4_scales)
+        xr_rows = xr.rearrange("(a p j) t -> a p j t", a=PASSES, j=PACK)
+        nc.sync.dma_start(out=xr0_raw[:], in_=xr_rows[0])
+        load_scale_rows(w4s, w4_scales)
+        for u in range(2):
+            nc.sync.dma_start(out=xr1_raw[u][:], in_=xr_rows[1][:, 2 * u : 2 * u + 2, :])
+
+        def deal_words(a):
+            nc.vector.tensor_copy(
+                out=x4[a][:].rearrange("p r (m b) -> p r m b", b=2),
+                in_=x4_raw[:, a, :].rearrange("p (m r b) -> p r m b", r=PACK, b=2),
+            )
+
+        deal_words(0)
+        nc.vector.tensor_copy(out=x4s[:], in_=x4s_raw[:].rearrange("p a (m r) -> p a r m", r=PACK))
+        deal_words(1)
+
+        def multiply(r, words, plane, a, first, last):
+            nc.tensor.matmul_mx(
+                out=acc[r][:],
+                lhsT=words,
+                lhsT_scale=plane,
+                rhs=w4[:, a, :].bitcast(FP4X4),
+                rhs_scale=w4s[:, a, :],
+                start=first,
+                stop=last,
+            )
+
+        for a in range(PASSES):
+            for r in range(PACK):
+                multiply(r, x4[a][:, r, :].bitcast(FP4X4), x4s[:, a, r, :], a, a == 0, False)
+
+        def round_xr(a, raw, slots):
+            src = raw[:].rearrange("p j (m r) -> p m j r", r=PACK)
+            dst = xr_bf[a][:, :, :, slots].rearrange("p r m j -> p m j r")
+            nc.vector.tensor_copy(out=dst[:, :XR_SPLIT], in_=src[:, :XR_SPLIT])
+            nc.scalar.copy(out=dst[:, XR_SPLIT:], in_=src[:, XR_SPLIT:])
+
+        round_xr(0, xr0_raw, slice(0, 4))
+        round_xr(1, xr1_raw[0], slice(0, 2))
+        nc.vector.quantize_mx(
+            out=xq[0][:].rearrange("p r m -> p (r m)").bitcast(FP8X4),
+            scales=xqs[0][:].rearrange("p r m -> p (r m)"),
+            in_=xr_bf[0][:].rearrange("p r m j -> p (r m j)"),
+        )
+        for r in range(PACK):
+            multiply(r, xq[0][:, r, :].bitcast(FP8X4), xqs[0][:, r, :], 0, False, False)
+        round_xr(1, xr1_raw[1], slice(2, 4))
+        for r in range(PACK):
+            nc.vector.quantize_mx(
+                out=xq[1][:, r, :].bitcast(FP8X4),
+                scales=xqs[1][:, r, :],
+                in_=xr_bf[1][:, r].rearrange("p m j -> p (m j)"),
+            )
+            multiply(r, xq[1][:, r, :].bitcast(FP8X4), xqs[1][:, r, :], 1, False, True)
+
+        out_rows = out_0.rearrange("(p r) n -> p r n", r=PACK)
+        for r in range(0, PACK, 2):
+            nc.vector.tensor_scalar(out=pos[r][:], in0=acc[r][:], scalar1=0.0, scalar2=None, op0=ALU.max)
+            nc.scalar.activation(out=pos[r + 1][:], in_=acc[r + 1][:], func=ACT.Relu)
+            nc.vector.tensor_tensor(out=res[:, r, :], in0=pos[r][:], in1=pos[r][:], op=ALU.mult)
+            nc.scalar.activation(out=res[:, r + 1, :], in_=pos[r + 1][:], func=ACT.Square)
+            nc.sync.dma_start(out=out_rows[:, r, :], in_=res[:, r, :])
+            nc.sync.dma_start(out=out_rows[:, r + 1, :], in_=res[:, r + 1, :])
+
+        half = N // 2
+        for h in range(2):
+            src = res[:, :, h * half : (h + 1) * half].rearrange("p r (c i) -> p c r i", i=4)
+            dst = res_bf[h][:].rearrange("p (c i) r -> p c r i", i=4)
+            cut = OUT_SPLIT // 4
+            nc.vector.tensor_copy(out=dst[:, :cut], in_=src[:, :cut])
+            nc.scalar.copy(out=dst[:, cut:], in_=src[:, cut:])
+        out_words = out_1[0].rearrange("p n i -> p (n i)").bitcast(I32)
+        for h in range(2):
+            cols = slice(h * half, (h + 1) * half)
+            nc.vector.quantize_mx(
+                out=codes[:, cols].bitcast(FP8X4),
+                scales=scales[:, cols],
+                in_=res_bf[h][:].rearrange("p n r -> p (n r)"),
+            )
+            nc.sync.dma_start(out=out_words[:, cols], in_=codes[:, cols].bitcast(I32))
+        for q in range(QUADS):
+            queue = nc.scalar if q % 2 else nc.sync
+            queue.dma_start(
+                out=out_2[0][4 * q : 4 * q + 4, :].bitcast(I32),
+                in_=scales[32 * q : 32 * q + 4, :].bitcast(I32),
+            )

@@ -20,7 +20,8 @@ PACK = 4
 PASSES = K // (P * PACK)
 QUADS = 4
 XR_SPLIT = 84
-OUT_SPLIT = 168
+WARM_PASSES = 3
+SQ_SPLIT = 128
 
 
 def tile_mix_xres_tm_pl_relu2_kernel(
@@ -44,30 +45,34 @@ def tile_mix_xres_tm_pl_relu2_kernel(
         xq = [sb.tile([P, PACK, P], U32, align_bytes=64, name="xq_%d" % a) for a in range(PASSES)]
         xqs = [sb.tile([P, PACK, P], U8, align_bytes=64, name="xqs_%d" % a) for a in range(PASSES)]
         acc = [psum.tile([P, N], F32, name="acc_%d" % r) for r in range(PACK)]
+        spare = psum.tile([P, N], F32)
         pos = [sb.tile([P, N], F32, align_bytes=64, name="pos_%d" % r) for r in range(PACK)]
         res = sb.tile([P, PACK, N], F32, align_bytes=64)
-        res_bf = [sb.tile([P, N // 2, PACK], BF16, align_bytes=64, name="res_bf_%d" % h) for h in range(2)]
+        res_bf = sb.tile([P, N, PACK], BF16, align_bytes=64)
+        warm = sb.tile([P, 2], F32)
         codes = sb.tile([P, N], U32, align_bytes=64)
         scales = sb.tile([P, N], U8, align_bytes=64)
 
-        def load_scale_rows(plane, rows):
+        def load_scale_rows(queue, plane, rows):
             for q in range(QUADS):
-                nc.scalar.dma_start(
+                queue.dma_start(
                     out=plane[32 * q : 32 * q + 4, :, :].bitcast(I32),
                     in_=rows[:, 4 * q : 4 * q + 4, :].rearrange("a s c -> s a c").bitcast(I32),
                 )
 
         nc.vector.memset(x4s_raw[:].bitcast(U32), 0)
         nc.vector.memset(w4s[:].bitcast(U32), 0)
+        nc.gpsimd.memset(warm[:, 0:1], 0.0)
 
         nc.sync.dma_start(out=x4_raw[:].bitcast(I32), in_=x4_words.rearrange("a p c -> p a c").bitcast(I32))
         nc.sync.dma_start(out=w4[:].bitcast(I32), in_=w4_words.rearrange("a p c -> p a c").bitcast(I32))
-        load_scale_rows(x4s_raw, x4_scales)
+        load_scale_rows(nc.sync, x4s_raw, x4_scales)
         xr_rows = xr.rearrange("(a p j) t -> a p j t", a=PASSES, j=PACK)
         nc.sync.dma_start(out=xr0_raw[:], in_=xr_rows[0])
-        load_scale_rows(w4s, w4_scales)
         for u in range(2):
             nc.sync.dma_start(out=xr1_raw[u][:], in_=xr_rows[1][:, 2 * u : 2 * u + 2, :])
+        nc.scalar.activation(out=warm[:, 1:2], in_=warm[:, 0:1], func=ACT.Square)
+        load_scale_rows(nc.scalar, w4s, w4_scales)
 
         def deal_words(a):
             nc.vector.tensor_copy(
@@ -90,18 +95,27 @@ def tile_mix_xres_tm_pl_relu2_kernel(
                 stop=last,
             )
 
+        for w in range(WARM_PASSES):
+            nc.tensor.matmul_mx(
+                out=spare[:],
+                lhsT=x4_raw[:, 0, : 2 * P].bitcast(FP4X4),
+                lhsT_scale=x4s_raw[:, 0, :P],
+                rhs=x4_raw[:, 0, :].bitcast(FP4X4),
+                rhs_scale=x4s_raw[:, 0, :],
+                start=True,
+                stop=True,
+            )
         for a in range(PASSES):
             for r in range(PACK):
                 multiply(r, x4[a][:, r, :].bitcast(FP4X4), x4s[:, a, r, :], a, a == 0, False)
 
-        def round_xr(a, raw, slots):
+        def round_xr(a, raw, slots, cut):
             src = raw[:].rearrange("p j (m r) -> p m j r", r=PACK)
             dst = xr_bf[a][:, :, :, slots].rearrange("p r m j -> p m j r")
-            nc.vector.tensor_copy(out=dst[:, :XR_SPLIT], in_=src[:, :XR_SPLIT])
-            nc.scalar.copy(out=dst[:, XR_SPLIT:], in_=src[:, XR_SPLIT:])
+            nc.vector.tensor_copy(out=dst[:, :cut], in_=src[:, :cut])
+            nc.scalar.copy(out=dst[:, cut:], in_=src[:, cut:])
 
-        round_xr(0, xr0_raw, slice(0, 4))
-        round_xr(1, xr1_raw[0], slice(0, 2))
+        round_xr(0, xr0_raw, slice(0, 4), XR_SPLIT)
         nc.vector.quantize_mx(
             out=xq[0][:].rearrange("p r m -> p (r m)").bitcast(FP8X4),
             scales=xqs[0][:].rearrange("p r m -> p (r m)"),
@@ -109,7 +123,8 @@ def tile_mix_xres_tm_pl_relu2_kernel(
         )
         for r in range(PACK):
             multiply(r, xq[0][:, r, :].bitcast(FP8X4), xqs[0][:, r, :], 0, False, False)
-        round_xr(1, xr1_raw[1], slice(2, 4))
+        round_xr(1, xr1_raw[0], slice(0, 2), P // 2)
+        round_xr(1, xr1_raw[1], slice(2, 4), XR_SPLIT)
         for r in range(PACK):
             nc.vector.quantize_mx(
                 out=xq[1][:, r, :].bitcast(FP8X4),
@@ -119,32 +134,46 @@ def tile_mix_xres_tm_pl_relu2_kernel(
             multiply(r, xq[1][:, r, :].bitcast(FP8X4), xqs[1][:, r, :], 1, False, True)
 
         out_rows = out_0.rearrange("(p r) n -> p r n", r=PACK)
-        for r in range(0, PACK, 2):
+        last = PACK - 1
+        nc.scalar.activation(out=pos[0][:], in_=acc[0][:], func=ACT.Relu)
+        for r in range(1, PACK):
             nc.vector.tensor_scalar(out=pos[r][:], in0=acc[r][:], scalar1=0.0, scalar2=None, op0=ALU.max)
-            nc.scalar.activation(out=pos[r + 1][:], in_=acc[r + 1][:], func=ACT.Relu)
-            nc.vector.tensor_tensor(out=res[:, r, :], in0=pos[r][:], in1=pos[r][:], op=ALU.mult)
-            nc.scalar.activation(out=res[:, r + 1, :], in_=pos[r + 1][:], func=ACT.Square)
+        for r in range(last):
+            nc.scalar.activation(out=res[:, r, :], in_=pos[r][:], func=ACT.Square)
             nc.sync.dma_start(out=out_rows[:, r, :], in_=res[:, r, :])
-            nc.sync.dma_start(out=out_rows[:, r + 1, :], in_=res[:, r + 1, :])
+        nc.scalar.activation(out=res[:, last, :SQ_SPLIT], in_=pos[last][:, :SQ_SPLIT], func=ACT.Square)
+        nc.vector.tensor_tensor(
+            out=res[:, last, SQ_SPLIT:], in0=pos[last][:, SQ_SPLIT:], in1=pos[last][:, SQ_SPLIT:], op=ALU.mult
+        )
+        nc.sync.dma_start(out=out_rows[:, last, :], in_=res[:, last, :])
 
-        half = N // 2
-        for h in range(2):
-            src = res[:, :, h * half : (h + 1) * half].rearrange("p r (c i) -> p c r i", i=4)
-            dst = res_bf[h][:].rearrange("p (c i) r -> p c r i", i=4)
-            cut = OUT_SPLIT // 4
-            nc.vector.tensor_copy(out=dst[:, :cut], in_=src[:, :cut])
-            nc.scalar.copy(out=dst[:, cut:], in_=src[:, cut:])
-        out_words = out_1[0].rearrange("p n i -> p (n i)").bitcast(I32)
-        for h in range(2):
-            cols = slice(h * half, (h + 1) * half)
+        def round_res(copy, cols):
+            copy(
+                out=res_bf[:, cols, :].rearrange("p (c i) r -> p c r i", i=4),
+                in_=res[:, :, cols].rearrange("p r (c i) -> p c r i", i=4),
+            )
+
+        def quantise_res(cols):
             nc.vector.quantize_mx(
                 out=codes[:, cols].bitcast(FP8X4),
                 scales=scales[:, cols],
-                in_=res_bf[h][:].rearrange("p n r -> p (n r)"),
+                in_=res_bf[:, cols, :].rearrange("p n r -> p (n r)"),
             )
-            nc.sync.dma_start(out=out_words[:, cols], in_=codes[:, cols].bitcast(I32))
+
+        quarters = [slice(c * P, (c + 1) * P) for c in range(4)]
+        halves = [slice(0, N // 2), slice(N // 2, N)]
+        round_res(nc.vector.tensor_copy, quarters[2])
+        round_res(nc.scalar.copy, quarters[0])
+        round_res(nc.vector.tensor_copy, quarters[3])
+        round_res(nc.scalar.copy, quarters[1])
+        out_words = out_1[0].rearrange("p n i -> p (n i)").bitcast(I32)
+        quantise_res(quarters[0])
+        quantise_res(halves[1])
+        nc.sync.dma_start(out=out_words[:, halves[1]], in_=codes[:, halves[1]].bitcast(I32))
+        quantise_res(quarters[1])
+        nc.sync.dma_start(out=out_words[:, halves[0]], in_=codes[:, halves[0]].bitcast(I32))
         for q in range(QUADS):
-            queue = nc.scalar if q % 2 else nc.sync
+            queue = nc.sync if q % 2 else nc.scalar
             queue.dma_start(
                 out=out_2[0][4 * q : 4 * q + 4, :].bitcast(I32),
                 in_=scales[32 * q : 32 * q + 4, :].bitcast(I32),

@@ -20,8 +20,8 @@ PACK = 4
 PASSES = K // (P * PACK)
 QUADS = 4
 XR_SPLIT = 84
-WARM_PASSES = 3
-SQ_SPLIT = 128
+WARM_PASSES = 4
+RES_SPLIT = 320
 
 
 def tile_mix_xres_tm_pl_relu2_kernel(
@@ -46,7 +46,7 @@ def tile_mix_xres_tm_pl_relu2_kernel(
         xqs = [sb.tile([P, PACK, P], U8, align_bytes=64, name="xqs_%d" % a) for a in range(PASSES)]
         acc = [psum.tile([P, N], F32, name="acc_%d" % r) for r in range(PACK)]
         spare = psum.tile([P, N], F32)
-        pos = [sb.tile([P, N], F32, align_bytes=64, name="pos_%d" % r) for r in range(PACK)]
+        pos = sb.tile([P, PACK, N], F32, align_bytes=64)
         res = sb.tile([P, PACK, N], F32, align_bytes=64)
         res_bf = sb.tile([P, N, PACK], BF16, align_bytes=64)
         warm = sb.tile([P, 2], F32)
@@ -69,10 +69,10 @@ def tile_mix_xres_tm_pl_relu2_kernel(
         load_scale_rows(nc.sync, x4s_raw, x4_scales)
         xr_rows = xr.rearrange("(a p j) t -> a p j t", a=PASSES, j=PACK)
         nc.sync.dma_start(out=xr0_raw[:], in_=xr_rows[0])
+        load_scale_rows(nc.sync, w4s, w4_scales)
         for u in range(2):
             nc.sync.dma_start(out=xr1_raw[u][:], in_=xr_rows[1][:, 2 * u : 2 * u + 2, :])
         nc.scalar.activation(out=warm[:, 1:2], in_=warm[:, 0:1], func=ACT.Square)
-        load_scale_rows(nc.scalar, w4s, w4_scales)
 
         def deal_words(a):
             nc.vector.tensor_copy(
@@ -121,7 +121,7 @@ def tile_mix_xres_tm_pl_relu2_kernel(
             scales=xqs[0][:].rearrange("p r m -> p (r m)"),
             in_=xr_bf[0][:].rearrange("p r m j -> p (r m j)"),
         )
-        for r in range(PACK):
+        for r in range(2):
             multiply(r, xq[0][:, r, :].bitcast(FP8X4), xqs[0][:, r, :], 0, False, False)
         round_xr(1, xr1_raw[0], slice(0, 2), P // 2)
         round_xr(1, xr1_raw[1], slice(2, 4), XR_SPLIT)
@@ -131,21 +131,32 @@ def tile_mix_xres_tm_pl_relu2_kernel(
                 scales=xqs[1][:, r, :],
                 in_=xr_bf[1][:, r].rearrange("p m j -> p (m j)"),
             )
+            if r >= 2:
+                multiply(r, xq[0][:, r, :].bitcast(FP8X4), xqs[0][:, r, :], 0, False, False)
             multiply(r, xq[1][:, r, :].bitcast(FP8X4), xqs[1][:, r, :], 1, False, True)
 
         out_rows = out_0.rearrange("(p r) n -> p r n", r=PACK)
         last = PACK - 1
-        nc.scalar.activation(out=pos[0][:], in_=acc[0][:], func=ACT.Relu)
-        for r in range(1, PACK):
-            nc.vector.tensor_scalar(out=pos[r][:], in0=acc[r][:], scalar1=0.0, scalar2=None, op0=ALU.max)
-        for r in range(last):
-            nc.scalar.activation(out=res[:, r, :], in_=pos[r][:], func=ACT.Square)
-            nc.sync.dma_start(out=out_rows[:, r, :], in_=res[:, r, :])
-        nc.scalar.activation(out=res[:, last, :SQ_SPLIT], in_=pos[last][:, :SQ_SPLIT], func=ACT.Square)
-        nc.vector.tensor_tensor(
-            out=res[:, last, SQ_SPLIT:], in0=pos[last][:, SQ_SPLIT:], in1=pos[last][:, SQ_SPLIT:], op=ALU.mult
-        )
-        nc.sync.dma_start(out=out_rows[:, last, :], in_=res[:, last, :])
+        lo, hi = slice(0, N // 2), slice(N // 2, N)
+
+        def relu_on_vector(r, cols):
+            nc.vector.tensor_scalar(out=pos[:, r, cols], in0=acc[r][:, cols], scalar1=0.0, scalar2=None, op0=ALU.max)
+
+        for cols in (lo, hi):
+            nc.scalar.activation(out=pos[:, 0, cols], in_=acc[0][:, cols], func=ACT.Relu)
+        for r in range(1, last):
+            relu_on_vector(r, slice(0, N))
+        relu_on_vector(last, hi)
+        relu_on_vector(last, lo)
+        for cols in (lo, hi):
+            nc.scalar.activation(out=res[:, 0, cols], in_=pos[:, 0, cols], func=ACT.Square)
+        nc.sync.dma_start(out=out_rows[:, 0, :], in_=res[:, 0, :])
+        nc.scalar.activation(out=res[:, 1, :], in_=pos[:, 1, :], func=ACT.Square)
+        nc.sync.dma_start(out=out_rows[:, 1, :], in_=res[:, 1, :])
+        for r in range(2, PACK):
+            nc.scalar.activation(out=res[:, r, lo], in_=pos[:, r, lo], func=ACT.Square)
+        nc.vector.tensor_tensor(out=res[:, 2:, hi], in0=pos[:, 2:, hi], in1=pos[:, 2:, hi], op=ALU.mult)
+        nc.sync.dma_start(out=out_rows[:, 2:, :], in_=res[:, 2:, :])
 
         def round_res(copy, cols):
             copy(
@@ -153,25 +164,17 @@ def tile_mix_xres_tm_pl_relu2_kernel(
                 in_=res[:, :, cols].rearrange("p r (c i) -> p c r i", i=4),
             )
 
-        def quantise_res(cols):
+        round_res(nc.vector.tensor_copy, lo)
+        round_res(nc.scalar.copy, slice(RES_SPLIT, N))
+        round_res(nc.vector.tensor_copy, slice(N // 2, RES_SPLIT))
+        out_words = out_1[0].rearrange("p n i -> p (n i)").bitcast(I32)
+        for cols in (lo, hi):
             nc.vector.quantize_mx(
                 out=codes[:, cols].bitcast(FP8X4),
                 scales=scales[:, cols],
                 in_=res_bf[:, cols, :].rearrange("p n r -> p (n r)"),
             )
-
-        quarters = [slice(c * P, (c + 1) * P) for c in range(4)]
-        halves = [slice(0, N // 2), slice(N // 2, N)]
-        round_res(nc.vector.tensor_copy, quarters[2])
-        round_res(nc.scalar.copy, quarters[0])
-        round_res(nc.vector.tensor_copy, quarters[3])
-        round_res(nc.scalar.copy, quarters[1])
-        out_words = out_1[0].rearrange("p n i -> p (n i)").bitcast(I32)
-        quantise_res(quarters[0])
-        quantise_res(halves[1])
-        nc.sync.dma_start(out=out_words[:, halves[1]], in_=codes[:, halves[1]].bitcast(I32))
-        quantise_res(quarters[1])
-        nc.sync.dma_start(out=out_words[:, halves[0]], in_=codes[:, halves[0]].bitcast(I32))
+            nc.sync.dma_start(out=out_words[:, cols], in_=codes[:, cols].bitcast(I32))
         for q in range(QUADS):
             queue = nc.sync if q % 2 else nc.scalar
             queue.dma_start(

@@ -19,8 +19,7 @@ P = 128
 PACK = 4
 PASSES = K // (P * PACK)
 QUADS = 4
-XR_SPLIT = 84
-WARM_PASSES = 4
+WARM_PASSES = 3
 RES_SPLIT = 320
 
 
@@ -49,12 +48,11 @@ def tile_mix_xres_tm_pl_relu2_kernel(
         pos = sb.tile([P, PACK, N], F32, align_bytes=64)
         res = sb.tile([P, PACK, N], F32, align_bytes=64)
         res_bf = sb.tile([P, N, PACK], BF16, align_bytes=64)
-        warm = sb.tile([P, 2], F32)
         codes = sb.tile([P, N], U32, align_bytes=64)
         scales = sb.tile([P, N], U8, align_bytes=64)
 
-        def load_scale_rows(queue, plane, rows):
-            for q in range(QUADS):
+        def load_scale_rows(queue, plane, rows, quads):
+            for q in quads:
                 queue.dma_start(
                     out=plane[32 * q : 32 * q + 4, :, :].bitcast(I32),
                     in_=rows[:, 4 * q : 4 * q + 4, :].rearrange("a s c -> s a c").bitcast(I32),
@@ -62,17 +60,15 @@ def tile_mix_xres_tm_pl_relu2_kernel(
 
         nc.vector.memset(x4s_raw[:].bitcast(U32), 0)
         nc.vector.memset(w4s[:].bitcast(U32), 0)
-        nc.gpsimd.memset(warm[:, 0:1], 0.0)
 
         nc.sync.dma_start(out=x4_raw[:].bitcast(I32), in_=x4_words.rearrange("a p c -> p a c").bitcast(I32))
         nc.sync.dma_start(out=w4[:].bitcast(I32), in_=w4_words.rearrange("a p c -> p a c").bitcast(I32))
-        load_scale_rows(nc.sync, x4s_raw, x4_scales)
+        load_scale_rows(nc.sync, x4s_raw, x4_scales, range(QUADS))
         xr_rows = xr.rearrange("(a p j) t -> a p j t", a=PASSES, j=PACK)
         nc.sync.dma_start(out=xr0_raw[:], in_=xr_rows[0])
-        load_scale_rows(nc.sync, w4s, w4_scales)
+        load_scale_rows(nc.sync, w4s, w4_scales, range(QUADS))
         for u in range(2):
             nc.sync.dma_start(out=xr1_raw[u][:], in_=xr_rows[1][:, 2 * u : 2 * u + 2, :])
-        nc.scalar.activation(out=warm[:, 1:2], in_=warm[:, 0:1], func=ACT.Square)
 
         def deal_words(a):
             nc.vector.tensor_copy(
@@ -109,31 +105,43 @@ def tile_mix_xres_tm_pl_relu2_kernel(
             for r in range(PACK):
                 multiply(r, x4[a][:, r, :].bitcast(FP4X4), x4s[:, a, r, :], a, a == 0, False)
 
-        def round_xr(a, raw, slots, cut):
-            src = raw[:].rearrange("p j (m r) -> p m j r", r=PACK)
-            dst = xr_bf[a][:, :, :, slots].rearrange("p r m j -> p m j r")
-            nc.vector.tensor_copy(out=dst[:, :cut], in_=src[:, :cut])
-            nc.scalar.copy(out=dst[:, cut:], in_=src[:, cut:])
-
-        round_xr(0, xr0_raw, slice(0, 4), XR_SPLIT)
-        nc.vector.quantize_mx(
-            out=xq[0][:].rearrange("p r m -> p (r m)").bitcast(FP8X4),
-            scales=xqs[0][:].rearrange("p r m -> p (r m)"),
-            in_=xr_bf[0][:].rearrange("p r m j -> p (r m j)"),
-        )
-        for r in range(2):
-            multiply(r, xq[0][:, r, :].bitcast(FP8X4), xqs[0][:, r, :], 0, False, False)
-        round_xr(1, xr1_raw[0], slice(0, 2), P // 2)
-        round_xr(1, xr1_raw[1], slice(2, 4), XR_SPLIT)
-        for r in range(PACK):
-            nc.vector.quantize_mx(
-                out=xq[1][:, r, :].bitcast(FP8X4),
-                scales=xqs[1][:, r, :],
-                in_=xr_bf[1][:, r].rearrange("p m j -> p (m j)"),
+        def round_xr(copy, a, raw, slots, rs):
+            copy(
+                out=xr_bf[a][:, rs, :, slots].rearrange("p r m j -> p m j r"),
+                in_=raw[:].rearrange("p j (m r) -> p m j r", r=PACK)[:, :, :, rs],
             )
+
+        def quantise_xr(a, rs):
+            nc.vector.quantize_mx(
+                out=xq[a][:, rs, :].rearrange("p r m -> p (r m)").bitcast(FP8X4),
+                scales=xqs[a][:, rs, :].rearrange("p r m -> p (r m)"),
+                in_=xr_bf[a][:, rs].rearrange("p r m j -> p (r m j)"),
+            )
+
+        def multiply_xr(r, a):
+            multiply(r, xq[a][:, r, :].bitcast(FP8X4), xqs[a][:, r, :], a, False, a == PASSES - 1)
+
+        def copy_by_table(out, in_):
+            nc.scalar.activation(out=out, in_=in_, func=ACT.Copy)
+
+        r01, r23 = slice(0, 2), slice(2, 4)
+        round_xr(nc.vector.tensor_copy, 0, xr0_raw, slice(0, 4), r01)
+        round_xr(copy_by_table, 0, xr0_raw, slice(0, 4), r23)
+        quantise_xr(0, r01)
+        round_xr(nc.vector.tensor_copy, 1, xr1_raw[0], slice(0, 2), r01)
+        round_xr(nc.scalar.copy, 1, xr1_raw[0], slice(0, 2), r23)
+        quantise_xr(0, r23)
+        round_xr(nc.vector.tensor_copy, 1, xr1_raw[1], slice(2, 4), r01)
+        round_xr(nc.vector.tensor_copy, 1, xr1_raw[1], slice(2, 4), slice(2, 3))
+        round_xr(nc.scalar.copy, 1, xr1_raw[1], slice(2, 4), slice(3, 4))
+        for r in range(PACK):
+            quantise_xr(1, slice(r, r + 1))
+        for r in range(2):
+            multiply_xr(r, 0)
+        for r in range(PACK):
             if r >= 2:
-                multiply(r, xq[0][:, r, :].bitcast(FP8X4), xqs[0][:, r, :], 0, False, False)
-            multiply(r, xq[1][:, r, :].bitcast(FP8X4), xqs[1][:, r, :], 1, False, True)
+                multiply_xr(r, 0)
+            multiply_xr(r, 1)
 
         out_rows = out_0.rearrange("(p r) n -> p r n", r=PACK)
         last = PACK - 1

from contextlib import ExitStack

import concourse.mybir as mybir

K, T, N = 1024, 512, 512
FLOPS = 2 * 2 * K * T * N

F32 = mybir.dt.float32
BF16 = mybir.dt.bfloat16
I32 = mybir.dt.int32
U32 = mybir.dt.uint32
U8 = mybir.dt.uint8
FP8X4 = mybir.dt.float8_e4m3fn_x4
FP4X4 = mybir.dt.float4_e2m1fn_x4
ALU = mybir.AluOpType
ACT = mybir.ActivationFunctionType

P = 128
PACK = 4
PASSES = K // (P * PACK)
QUADS = 4
WARM_PASSES = 3
RES_SPLIT = 320


def tile_mix_xres_tm_pl_relu2_kernel(
    tc, x4_words, x4_scales, xr, w4_words, w4_scales, out_0, out_1, out_2
):
    nc = tc.nc
    with ExitStack() as ctx:
        sb = ctx.enter_context(tc.tile_pool(name="sb", bufs=1))
        psum = ctx.enter_context(tc.psum_pool(name="psum", bufs=1))
        ctx.enter_context(tc.manual_schedule())

        x4_raw = sb.tile([P, PASSES, 2 * T], U8, align_bytes=64)
        x4s_raw = sb.tile([P, PASSES, T], U8, align_bytes=64)
        w4 = sb.tile([P, PASSES, 2 * N], U8, align_bytes=64)
        w4s = sb.tile([P, PASSES, N], U8, align_bytes=64)
        x4 = [sb.tile([P, PACK, 2 * P], U8, align_bytes=64, name="x4_%d" % a) for a in range(PASSES)]
        x4s = sb.tile([P, PASSES, PACK, P], U8, align_bytes=64)
        xr0_raw = sb.tile([P, PACK, T], F32, align_bytes=64)
        xr1_raw = [sb.tile([P, 2, T], F32, align_bytes=64, name="xr1_raw_%d" % u) for u in range(2)]
        xr_bf = [sb.tile([P, PACK, P, PACK], BF16, align_bytes=64, name="xr_bf_%d" % a) for a in range(PASSES)]
        xq = [sb.tile([P, PACK, P], U32, align_bytes=64, name="xq_%d" % a) for a in range(PASSES)]
        xqs = [sb.tile([P, PACK, P], U8, align_bytes=64, name="xqs_%d" % a) for a in range(PASSES)]
        acc = [psum.tile([P, N], F32, name="acc_%d" % r) for r in range(PACK)]
        spare = psum.tile([P, N], F32)
        pos = sb.tile([P, PACK, N], F32, align_bytes=64)
        res = sb.tile([P, PACK, N], F32, align_bytes=64)
        res_bf = sb.tile([P, N, PACK], BF16, align_bytes=64)
        codes = sb.tile([P, N], U32, align_bytes=64)
        scales = sb.tile([P, N], U8, align_bytes=64)

        def load_scale_rows(queue, plane, rows, quads):
            for q in quads:
                queue.dma_start(
                    out=plane[32 * q : 32 * q + 4, :, :].bitcast(I32),
                    in_=rows[:, 4 * q : 4 * q + 4, :].rearrange("a s c -> s a c").bitcast(I32),
                )

        nc.vector.memset(x4s_raw[:].bitcast(U32), 0)
        nc.vector.memset(w4s[:].bitcast(U32), 0)

        nc.sync.dma_start(out=x4_raw[:].bitcast(I32), in_=x4_words.rearrange("a p c -> p a c").bitcast(I32))
        nc.sync.dma_start(out=w4[:].bitcast(I32), in_=w4_words.rearrange("a p c -> p a c").bitcast(I32))
        load_scale_rows(nc.sync, x4s_raw, x4_scales, range(QUADS))
        xr_rows = xr.rearrange("(a p j) t -> a p j t", a=PASSES, j=PACK)
        nc.sync.dma_start(out=xr0_raw[:], in_=xr_rows[0])
        load_scale_rows(nc.sync, w4s, w4_scales, range(QUADS))
        for u in range(2):
            nc.sync.dma_start(out=xr1_raw[u][:], in_=xr_rows[1][:, 2 * u : 2 * u + 2, :])

        def deal_words(a):
            nc.vector.tensor_copy(
                out=x4[a][:].rearrange("p r (m b) -> p r m b", b=2),
                in_=x4_raw[:, a, :].rearrange("p (m r b) -> p r m b", r=PACK, b=2),
            )

        deal_words(0)
        nc.vector.tensor_copy(out=x4s[:], in_=x4s_raw[:].rearrange("p a (m r) -> p a r m", r=PACK))
        deal_words(1)

        def multiply(r, words, plane, a, first, last):
            nc.tensor.matmul_mx(
                out=acc[r][:],
                lhsT=words,
                lhsT_scale=plane,
                rhs=w4[:, a, :].bitcast(FP4X4),
                rhs_scale=w4s[:, a, :],
                start=first,
                stop=last,
            )

        for w in range(WARM_PASSES):
            nc.tensor.matmul_mx(
                out=spare[:],
                lhsT=x4_raw[:, 0, : 2 * P].bitcast(FP4X4),
                lhsT_scale=x4s_raw[:, 0, :P],
                rhs=x4_raw[:, 0, :].bitcast(FP4X4),
                rhs_scale=x4s_raw[:, 0, :],
                start=True,
                stop=True,
            )
        for a in range(PASSES):
            for r in range(PACK):
                multiply(r, x4[a][:, r, :].bitcast(FP4X4), x4s[:, a, r, :], a, a == 0, False)

        def round_xr(copy, a, raw, slots, rs):
            copy(
                out=xr_bf[a][:, rs, :, slots].rearrange("p r m j -> p m j r"),
                in_=raw[:].rearrange("p j (m r) -> p m j r", r=PACK)[:, :, :, rs],
            )

        def quantise_xr(a, rs):
            nc.vector.quantize_mx(
                out=xq[a][:, rs, :].rearrange("p r m -> p (r m)").bitcast(FP8X4),
                scales=xqs[a][:, rs, :].rearrange("p r m -> p (r m)"),
                in_=xr_bf[a][:, rs].rearrange("p r m j -> p (r m j)"),
            )

        def multiply_xr(r, a):
            multiply(r, xq[a][:, r, :].bitcast(FP8X4), xqs[a][:, r, :], a, False, a == PASSES - 1)

        def copy_by_table(out, in_):
            nc.scalar.activation(out=out, in_=in_, func=ACT.Copy)

        r01, r23 = slice(0, 2), slice(2, 4)
        round_xr(nc.vector.tensor_copy, 0, xr0_raw, slice(0, 4), r01)
        round_xr(copy_by_table, 0, xr0_raw, slice(0, 4), r23)
        quantise_xr(0, r01)
        round_xr(nc.vector.tensor_copy, 1, xr1_raw[0], slice(0, 2), r01)
        round_xr(nc.scalar.copy, 1, xr1_raw[0], slice(0, 2), r23)
        quantise_xr(0, r23)
        round_xr(nc.vector.tensor_copy, 1, xr1_raw[1], slice(2, 4), r01)
        round_xr(nc.vector.tensor_copy, 1, xr1_raw[1], slice(2, 4), slice(2, 3))
        round_xr(nc.scalar.copy, 1, xr1_raw[1], slice(2, 4), slice(3, 4))
        for r in range(PACK):
            quantise_xr(1, slice(r, r + 1))
        for r in range(2):
            multiply_xr(r, 0)
        for r in range(PACK):
            if r >= 2:
                multiply_xr(r, 0)
            multiply_xr(r, 1)

        out_rows = out_0.rearrange("(p r) n -> p r n", r=PACK)
        last = PACK - 1
        lo, hi = slice(0, N // 2), slice(N // 2, N)

        def relu_on_vector(r, cols):
            nc.vector.tensor_scalar(out=pos[:, r, cols], in0=acc[r][:, cols], scalar1=0.0, scalar2=None, op0=ALU.max)

        for cols in (lo, hi):
            nc.scalar.activation(out=pos[:, 0, cols], in_=acc[0][:, cols], func=ACT.Relu)
        for r in range(1, last):
            relu_on_vector(r, slice(0, N))
        relu_on_vector(last, hi)
        relu_on_vector(last, lo)
        for cols in (lo, hi):
            nc.scalar.activation(out=res[:, 0, cols], in_=pos[:, 0, cols], func=ACT.Square)
        nc.sync.dma_start(out=out_rows[:, 0, :], in_=res[:, 0, :])
        nc.scalar.activation(out=res[:, 1, :], in_=pos[:, 1, :], func=ACT.Square)
        nc.sync.dma_start(out=out_rows[:, 1, :], in_=res[:, 1, :])
        for r in range(2, PACK):
            nc.scalar.activation(out=res[:, r, lo], in_=pos[:, r, lo], func=ACT.Square)
        nc.vector.tensor_tensor(out=res[:, 2:, hi], in0=pos[:, 2:, hi], in1=pos[:, 2:, hi], op=ALU.mult)
        nc.sync.dma_start(out=out_rows[:, 2:, :], in_=res[:, 2:, :])

        def round_res(copy, cols):
            copy(
                out=res_bf[:, cols, :].rearrange("p (c i) r -> p c r i", i=4),
                in_=res[:, :, cols].rearrange("p r (c i) -> p c r i", i=4),
            )

        round_res(nc.vector.tensor_copy, lo)
        round_res(nc.scalar.copy, slice(RES_SPLIT, N))
        round_res(nc.vector.tensor_copy, slice(N // 2, RES_SPLIT))
        out_words = out_1[0].rearrange("p n i -> p (n i)").bitcast(I32)
        for cols in (lo, hi):
            nc.vector.quantize_mx(
                out=codes[:, cols].bitcast(FP8X4),
                scales=scales[:, cols],
                in_=res_bf[:, cols, :].rearrange("p n r -> p (n r)"),
            )
            nc.sync.dma_start(out=out_words[:, cols], in_=codes[:, cols].bitcast(I32))
        for q in range(QUADS):
            queue = nc.sync if q % 2 else nc.scalar
            queue.dma_start(
                out=out_2[0][4 * q : 4 * q + 4, :].bitcast(I32),
                in_=scales[32 * q : 32 * q + 4, :].bitcast(I32),
            )
